import numpy as np
import ml_dtypes


def mxq(x, axis, fmt="e4m3"):
    dtype, down = {"e4m3": (ml_dtypes.float8_e4m3fn, 7), "e5m2": (ml_dtypes.float8_e5m2, 14)}[fmt]
    v = np.moveaxis(np.asarray(x, np.float32).astype(ml_dtypes.bfloat16).astype(np.float64), axis, -1)
    blocks = v.reshape(v.shape[:-1] + (-1, 32))
    amax = np.abs(blocks).max(-1, keepdims=True)
    byte = np.maximum(np.where(amax > 0, np.frexp(amax)[1] - 1 + 127, 0) - down, 1)
    scale = np.exp2(byte - 127.0)
    codes = (blocks / scale).astype(np.float32).astype(dtype).astype(np.float64)
    return np.moveaxis((codes * scale).reshape(v.shape), -1, axis)


WIDE = False


def mx_kscale(k):
    if not WIDE:
        return np.ones(k)
    levels = np.array([10, -10, 5, -5, 0])
    if k % 512:
        return np.exp2(np.random.permutation(np.resize(levels, k // 32))).repeat(32)
    a = np.empty((k // 512, 16))
    for p in range(k // 512):
        a[p, :8] = np.random.permutation(np.resize(levels, 8))
        for g in range(8):
            far = levels[np.abs(levels - a[p, g]) >= 10]
            a[p, g + 8] = far[np.random.randint(len(far))]
    return np.exp2(a.ravel()).repeat(32)


def f64(x):
    return np.asarray(x).astype(np.float64)


def striped(idx):
    return np.tile(idx.reshape(-1, 16).T, (8, 1)).astype(np.uint16)


def unstriped(offs):
    return offs[:16].T.reshape(-1).astype(np.int64)


E2M1 = np.array([0.0, 0.5, 1.0, 1.5, 2.0, 3.0, 4.0, 6.0, -0.0, -0.5, -1.0, -1.5, -2.0, -3.0, -4.0, -6.0])


def pack_weight(w, fmt):
    k, n = w.shape
    w = f64(np.asarray(w, np.float32).astype(ml_dtypes.bfloat16)).reshape(k // 32, 32, n)
    amax = np.abs(w).max(1)
    if fmt == "e4m3":
        byte = np.frexp(amax)[1] - 1 + 127 - 7
    else:
        mant, ex = np.frexp(amax / 6.0)
        byte = np.where(mant > 0.5, ex, ex - 1) + 127
    byte = np.clip(np.where(amax > 0, byte, 1), 1, 254)
    scaled = (w * np.exp2(127.0 - byte)[:, None, :]).reshape(k, n).astype(np.float32)
    by_word = np.ascontiguousarray(scaled.reshape(k // 512, 128, 4, n).transpose(0, 1, 3, 2))
    if fmt == "e4m3":
        words = by_word.astype(ml_dtypes.float8_e4m3fn).view(np.uint8)
    else:
        c = by_word.astype(ml_dtypes.float4_e2m1fn).view(np.uint8) & 0xF
        words = (c[..., 0::2] | (c[..., 1::2] << 4)).reshape(k // 512, 128, 2 * n)
    return np.ascontiguousarray(words), np.ascontiguousarray(byte.astype(np.uint8).reshape(k // 512, 16, n))


def unpack_weight(words, scales, fmt):
    g, _, n = scales.shape
    words = np.ascontiguousarray(words).reshape(g, 128, n, -1)
    if fmt == "e4m3":
        vals = words.view(ml_dtypes.float8_e4m3fn).astype(np.float64)
    else:
        nib = np.empty((g, 128, n, 4), np.uint8)
        nib[..., 0::2] = words & 0xF
        nib[..., 1::2] = words >> 4
        vals = E2M1[nib]
    vals = vals * np.repeat(np.exp2(scales.astype(np.float64) - 127.0), 8, axis=1)[..., None]
    return vals.transpose(0, 1, 3, 2).reshape(g * 512, n)


def gelu(v):
    return 0.5 * v * (1.0 + np.tanh(np.sqrt(2.0 / np.pi) * (v + 0.044715 * v**3)))


K, K2, H, N, T, S = 1024, 512, 1024, 512, 4096, 1024

def setup_inputs():
    n = np.random.standard_normal
    s = mx_kscale(K)[:, None]
    s2 = mx_kscale(K2)[:, None]
    u = mx_kscale(H)[:, None]
    d = {}
    d["tab_words"], d["tab_scales"] = pack_weight(n((K, T)) * s, "e4m3")
    d["offs"] = striped(np.random.permutation(T)[:S])
    d["xs_words"], d["xs_scales"] = pack_weight(n((K2, S)) * s2, "e4m3")
    d["w1_words"], d["w1_scales"] = pack_weight(n((K, H)) / s * u.T / K ** 0.5, "e2m1")
    d["w2"] = (n((K2, H)) / s2 * u.T / K2 ** 0.5).astype(np.float32)
    d["w3"] = (1.5 * n((H, N)) / u / H ** 0.5).astype(np.float32)
    d["gain"] = np.exp(0.4 * n(N)).astype(np.float32)
    return d

def reference(tab_words, tab_scales, offs, xs_words, xs_scales, w1_words, w1_scales, w2, w3, gain):
    v = unpack_weight(tab_words, tab_scales, "e4m3")[:, unstriped(offs)]
    xs = unpack_weight(xs_words, xs_scales, "e4m3")
    w1 = unpack_weight(w1_words, w1_scales, "e2m1")
    h1 = np.abs(w1.T @ v)
    h2 = np.abs(mxq(f64(w2), 0, "e4m3").T @ xs)
    z = np.minimum(h1, h2)
    y = mxq(f64(w3), 0, "e4m3").T @ mxq(z, 0, "e4m3")
    return f64(gain)[:, None] * y

@@ -1,0 +1,229 @@
+from contextlib import ExitStack
+
+import concourse.mybir as mybir
+
+K, K2, H, N, T, S = 1024, 512, 1024, 512, 4096, 1024
+FLOPS = 2 * S * (K * H + K2 * H + H * N)
+
+F32 = mybir.dt.float32
+BF16 = mybir.dt.bfloat16
+I32 = mybir.dt.int32
+U32 = mybir.dt.uint32
+U16 = mybir.dt.uint16
+U8 = mybir.dt.uint8
+FP8X4 = mybir.dt.float8_e4m3fn_x4
+FP4X4 = mybir.dt.float4_e2m1fn_x4
+ABS = mybir.ActivationFunctionType.Abs
+COPY = mybir.ActivationFunctionType.Copy
+MIN = mybir.AluOpType.min
+MULT = mybir.AluOpType.mult
+
+P = 128
+PACK = 4
+K_PASS = P * PACK
+K_PASSES = K // K_PASS
+R_PASSES = H // K_PASS
+N_TILES = N // P
+UNIT = 128
+HALF = S // 2
+CHUNKS = (256, 256, 256, 128, 128)
+VECTOR_CHUNKS = 2
+LAG = 5
+
+
+def tile_list_cork_taint_overlap_kernel(
+    tc, tab_words, tab_scales, offs, xs_words, xs_scales, w1_words, w1_scales, w2, w3, gain, out
+):
+    nc = tc.nc
+    with ExitStack() as ctx:
+        lists = ctx.enter_context(tc.tile_pool(name="lists", bufs=1))
+        keep = ctx.enter_context(tc.tile_pool(name="keep", bufs=1))
+        stage = ctx.enter_context(tc.tile_pool(name="stage", bufs=2))
+        psum = ctx.enter_context(tc.psum_pool(name="psum", bufs=8))
+
+        offsets = lists.tile([P, S // 16], U16, name="offsets")
+        nc.sync.dma_start(offsets[:], offs)
+
+        rows = K_PASSES * 16
+        xs_plane = keep.tile([P, S], U8, name="xs_plane", align_bytes=64)
+        nc.vector.memset(xs_plane[:].bitcast(I32), 0)
+        w1_rows = keep.tile([P, H], U8, name="w1_rows", align_bytes=64)
+        nc.sync.dma_start(w1_rows[0:rows, :].bitcast(I32), w1_scales.rearrange("a q c -> (a q) c").bitcast(I32))
+        tab_rows = keep.tile([P, T], U8, name="tab_rows", align_bytes=64)
+        nc.sync.dma_start(tab_rows[0:rows, :].bitcast(I32), tab_scales.rearrange("a q c -> (a q) c").bitcast(I32))
+        nc.vector.memset(tab_rows[32:64, :].bitcast(I32), 0)
+        nc.vector.memset(tab_rows[64:128, :].bitcast(I32), 0)
+        planes = keep.tile([P, K_PASSES, S + H], U8, name="planes", align_bytes=64)
+        nc.vector.memset(planes[:].rearrange("p a c -> p (a c)").bitcast(I32), 0)
+
+
+        def load_w2(b):
+            raw = stage.tile([P, PACK, K_PASS], F32, name="raw", align_bytes=64)
+            nc.sync.dma_start(raw[:], w2[:, b * K_PASS : (b + 1) * K_PASS].rearrange("(p i) c -> p i c", i=PACK))
+            return raw
+
+        w2_raw = [load_w2(0)]
+        for quadrant in range(4):
+            nc.sync.dma_start(
+                xs_plane[32 * quadrant : 32 * quadrant + 4, :].bitcast(I32),
+                xs_scales[0, 4 * quadrant : 4 * quadrant + 4, :].bitcast(I32),
+            )
+        xs_codes = keep.tile([P, S], I32, name="xs_codes", align_bytes=64)
+        nc.sync.dma_start(xs_codes[:], xs_words[0].rearrange("p c i -> p (c i)").bitcast(I32))
+        w2_raw.append(load_w2(1))
+        w1_raw = keep.tile([P, K_PASSES, H // 2], I32, name="w1_raw", align_bytes=64)
+        nc.sync.dma_start(w1_raw[:], w1_words.rearrange("a p c -> p a c").bitcast(I32))
+
+        gains = keep.tile([P, N_TILES], F32, name="gains")
+        with nc.allow_non_contiguous_dma(reason="one gain a partition"):
+            nc.sync.dma_start(gains[:], gain.rearrange("(i p) -> p i", p=P))
+
+        joined = keep.tile([P, (S + H) // 4], I32, name="joined", align_bytes=64)
+        nc.vector.tensor_copy(
+            joined[0:rows, S // 4 :].rearrange("p (b t g w) -> p b t g w", b=R_PASSES, t=PACK, w=2),
+            w1_rows[0:rows, :].bitcast(I32).rearrange("p (b g t w) -> p b t g w", b=R_PASSES, t=PACK, w=2),
+        )
+        picked_rows = keep.tile([P, S], U8, name="picked_rows", tag="table", align_bytes=64)
+        nc.vector.tensor_copy(picked_rows[:], tab_rows[:].indirect(offsets[:]))
+        nc.vector.tensor_copy(joined[0:rows, 0 : S // 4], picked_rows[0:rows, :].bitcast(I32))
+
+        table = keep.tile([P, K_PASSES, T], I32, name="table", tag="table", align_bytes=64)
+        for a in range(K_PASSES):
+            for quadrant in range(4):
+                first = 16 * a + 4 * quadrant
+                nc.sync.dma_start(
+                    planes[32 * quadrant : 32 * quadrant + 4, a, :].bitcast(I32), joined[first : first + 4, :]
+                )
+            nc.sync.dma_start(table[:, a, :], tab_words[a].rearrange("p c i -> p (c i)").bitcast(I32))
+
+        starts = [sum(CHUNKS[:c]) for c in range(len(CHUNKS))]
+        units = [(c, u) for c, width in enumerate(CHUNKS) for u in range(width // UNIT)]
+
+        def abs_out(target, bank):
+            nc.scalar.activation(
+                target.rearrange("p (j t) -> p j t", t=PACK), bank[:].rearrange("p (t j) -> p j t", t=PACK), ABS
+            )
+
+        h2 = [keep.tile([P, R_PASSES, PACK * width], BF16, name="h2_%d" % c, align_bytes=64) for c, width in enumerate(CHUNKS)]
+        for b in range(R_PASSES):
+            w2_bf = stage.tile([P, PACK * K_PASS], BF16, name="w_bf", align_bytes=64)
+            nc.vector.tensor_copy(
+                w2_bf[:].rearrange("p (t g q i) -> p t g i q", t=PACK, q=8, i=PACK),
+                w2_raw[b][:].rearrange("p i (g t q) -> p t g i q", t=PACK, q=8),
+            )
+            w2_codes = keep.tile([P, K_PASS], U32, name="w2_codes_%d" % b, align_bytes=64)
+            w2_plane = keep.tile([P, K_PASS], U8, name="w2_plane_%d" % b, align_bytes=64)
+            nc.vector.quantize_mx(out=w2_codes[:].bitcast(FP8X4), scales=w2_plane[:], in_=w2_bf[:])
+            for c, u in units:
+                tokens = slice(starts[c] + u * UNIT, starts[c] + (u + 1) * UNIT)
+                bank = psum.tile([P, PACK * UNIT], F32, name="bank")
+                for t in range(PACK):
+                    cols = slice(t * P, (t + 1) * P)
+                    nc.tensor.matmul_mx(
+                        out=bank[:, t * UNIT : (t + 1) * UNIT],
+                        lhsT=w2_codes[:, cols].bitcast(FP8X4),
+                        lhsT_scale=w2_plane[:, cols],
+                        rhs=xs_codes[:, tokens].bitcast(FP8X4),
+                        rhs_scale=xs_plane[:, tokens],
+                        start=True,
+                        stop=True,
+                    )
+                abs_out(h2[c][:, b, u * PACK * UNIT : (u + 1) * PACK * UNIT], bank)
+
+        w1_codes = keep.tile([P, K_PASSES * H // 2], I32, name="w1_codes", align_bytes=64)
+        nc.vector.tensor_copy(
+            w1_codes[:].rearrange("p (e t g w) -> p e t g w", t=PACK, g=16, w=4),
+            w1_raw[:].rearrange("p a (b g t w) -> p (a b) t g w", b=R_PASSES, t=PACK, w=4),
+        )
+
+        picked = {}
+        for a in range(K_PASSES):
+            for half in range(2):
+                words = keep.tile([P, HALF], U32, name="picked_%d_%d" % (a, half), align_bytes=64)
+                entries = offsets[:, half * HALF // 16 : (half + 1) * HALF // 16]
+                nc.vector.tensor_copy(words[:], table[:, a, :].bitcast(U32).indirect(entries))
+                picked[a, half] = words
+
+        w3_codes = []
+        w3_planes = []
+        for b in range(R_PASSES):
+            raw = stage.tile([P, PACK, N], F32, name="raw", align_bytes=64)
+            by_slot = w3[b * K_PASS : (b + 1) * K_PASS, :].rearrange("(g t q) n -> t g q n", t=PACK, q=8)
+            for t in range(PACK):
+                nc.sync.dma_start(raw[:, t, :], by_slot[t])
+            w3_bf = stage.tile([P, PACK * N], BF16, name="w_bf", align_bytes=64)
+            nc.vector.tensor_copy(
+                w3_bf[:].rearrange("p (c i t) -> p c t i", i=4, t=PACK),
+                raw[:].rearrange("p t (c i) -> p c t i", i=4),
+            )
+            codes = keep.tile([P, N], U32, name="w3_codes_%d" % b, align_bytes=64)
+            plane = keep.tile([P, N], U8, name="w3_plane_%d" % b, align_bytes=64)
+            nc.vector.quantize_mx(out=codes[:].bitcast(FP8X4), scales=plane[:], in_=w3_bf[:])
+            w3_codes.append(codes)
+            w3_planes.append(plane)
+
+        h1 = [keep.tile([P, R_PASSES, PACK * width], BF16, name="h1_%d" % c, align_bytes=64) for c, width in enumerate(CHUNKS)]
+        z_codes = []
+        z_planes = []
+
+        def overlap(c):
+            width = CHUNKS[c]
+            for u in range(width // UNIT):
+                token = starts[c] + u * UNIT
+                half, place = divmod(token, HALF)
+                for b in range(R_PASSES):
+                    bank = psum.tile([P, PACK * UNIT], F32, name="bank")
+                    for a in range(K_PASSES):
+                        for t in range(PACK):
+                            column = b * K_PASS + t * P
+                            word = (a * H + column) // 2
+                            nc.tensor.matmul_mx(
+                                out=bank[:, t * UNIT : (t + 1) * UNIT],
+                                lhsT=w1_codes[:, word : word + P // 2].bitcast(FP4X4),
+                                lhsT_scale=planes[:, a, S + column : S + column + P],
+                                rhs=picked[a, half][:, place : place + UNIT].bitcast(FP8X4),
+                                rhs_scale=planes[:, a, token : token + UNIT],
+                                start=(a == 0 and t == 0),
+                                stop=(a == K_PASSES - 1 and t == PACK - 1),
+                            )
+                    abs_out(h1[c][:, b, u * PACK * UNIT : (u + 1) * PACK * UNIT], bank)
+            z = keep.tile([P, R_PASSES, PACK * width], BF16, name="z_%d" % c, align_bytes=64)
+            nc.vector.tensor_tensor(z[:], h1[c][:], h2[c][:], MIN)
+            codes = keep.tile([P, R_PASSES * width], U32, name="z_codes_%d" % c, align_bytes=64)
+            plane = keep.tile([P, R_PASSES * width], U8, name="z_plane_%d" % c, align_bytes=64)
+            nc.vector.quantize_mx(out=codes[:].bitcast(FP8X4), scales=plane[:], in_=z[:].rearrange("p b c -> p (b c)"))
+            z_codes.append(codes)
+            z_planes.append(plane)
+
+        out_rows = out.rearrange("(i p) j -> p i j", p=P)
+
+        def scores(c):
+            width = CHUNKS[c]
+            result = keep.tile([P, N_TILES, width], F32, name="result_%d" % c, align_bytes=64)
+            per_bank = 2
+            for first in range(0, N_TILES, per_bank):
+                bank = psum.tile([P, PACK * UNIT], F32, name="bank")
+                for i in range(first, first + per_bank):
+                    for b in range(R_PASSES):
+                        nc.tensor.matmul_mx(
+                            out=bank[:, (i - first) * width : (i - first + 1) * width],
+                            lhsT=w3_codes[b][:, i * P : (i + 1) * P].bitcast(FP8X4),
+                            lhsT_scale=w3_planes[b][:, i * P : (i + 1) * P],
+                            rhs=z_codes[c][:, b * width : (b + 1) * width].bitcast(FP8X4),
+                            rhs_scale=z_planes[c][:, b * width : (b + 1) * width],
+                            start=(b == 0),
+                            stop=(b == R_PASSES - 1),
+                        )
+                for i in range(first, first + per_bank):
+                    sums = bank[:, (i - first) * width : (i - first + 1) * width]
+                    if c >= len(CHUNKS) - VECTOR_CHUNKS:
+                        nc.vector.tensor_scalar(result[:, i, :], sums, gains[:, i : i + 1], None, MULT)
+                    else:
+                        nc.scalar.activation(result[:, i, :], sums, COPY, scale=gains[:, i : i + 1])
+            nc.sync.dma_start(out_rows[:, :, starts[c] : starts[c] + width], result[:])
+
+        for c in range(len(CHUNKS) + LAG):
+            if c < len(CHUNKS):
+                overlap(c)
+            if c >= LAG:
+                scores(c - LAG)

@@ -101,7 +101,9 @@ def tile_list_cork_taint_overlap_kernel(
 
         def abs_out(target, bank):
             nc.scalar.activation(
-                target.rearrange("p (j t) -> p j t", t=PACK), bank[:].rearrange("p (t j) -> p j t", t=PACK), ABS
+                target.rearrange("p (j e t) -> p j t e", t=PACK, e=2),
+                bank[:].rearrange("p (t j e) -> p j t e", t=PACK, e=2),
+                ABS,
             )
 
         h2 = [keep.tile([P, R_PASSES, PACK * width], BF16, name="h2_%d" % c, align_bytes=64) for c, width in enumerate(CHUNKS)]

@@ -19,16 +19,22 @@ MIN = mybir.AluOpType.min
 MULT = mybir.AluOpType.mult
 
 P = 128
+QUADRANT = 32
+LIVE_ROWS = 4
 PACK = 4
 K_PASS = P * PACK
+BLOCKS = K_PASS // 32
 K_PASSES = K // K_PASS
 R_PASSES = H // K_PASS
 N_TILES = N // P
-UNIT = 128
+LIST_ROWS = 16
+BANKS = 8
+BANK_COLUMNS = 512
+UNIT = BANK_COLUMNS // PACK
 HALF = S // 2
 CHUNKS = (256, 256, 256, 128, 128)
-VECTOR_CHUNKS = 2
-LAG = 5
+TILES_PER_BANK = 2
+SHARED_CHUNKS = 2
 
 
 def tile_list_cork_taint_overlap_kernel(
@@ -38,158 +44,168 @@ def tile_list_cork_taint_overlap_kernel(
     with ExitStack() as ctx:
         lists = ctx.enter_context(tc.tile_pool(name="lists", bufs=1))
         keep = ctx.enter_context(tc.tile_pool(name="keep", bufs=1))
-        stage = ctx.enter_context(tc.tile_pool(name="stage", bufs=2))
-        psum = ctx.enter_context(tc.psum_pool(name="psum", bufs=8))
+        ring = ctx.enter_context(tc.tile_pool(name="ring", bufs=2))
+        psum = ctx.enter_context(tc.psum_pool(name="psum", bufs=1))
 
-        offsets = lists.tile([P, S // 16], U16, name="offsets")
+        offsets = lists.tile([P, S // LIST_ROWS], U16, name="offsets")
         nc.sync.dma_start(offsets[:], offs)
 
-        rows = K_PASSES * 16
         xs_plane = keep.tile([P, S], U8, name="xs_plane", align_bytes=64)
         nc.vector.memset(xs_plane[:].bitcast(I32), 0)
-        w1_rows = keep.tile([P, H], U8, name="w1_rows", align_bytes=64)
-        nc.sync.dma_start(w1_rows[0:rows, :].bitcast(I32), w1_scales.rearrange("a q c -> (a q) c").bitcast(I32))
+
+        scale_rows = K_PASSES * BLOCKS
+        w1_rows = keep.tile([P, H], U8, name="w1_rows", tag="late_table", align_bytes=64)
         tab_rows = keep.tile([P, T], U8, name="tab_rows", align_bytes=64)
-        nc.sync.dma_start(tab_rows[0:rows, :].bitcast(I32), tab_scales.rearrange("a q c -> (a q) c").bitcast(I32))
-        nc.vector.memset(tab_rows[32:64, :].bitcast(I32), 0)
-        nc.vector.memset(tab_rows[64:128, :].bitcast(I32), 0)
+        for tile, scales in ((tab_rows, tab_scales), (w1_rows, w1_scales)):
+            nc.sync.dma_start(tile[0:scale_rows, :].bitcast(I32), scales.rearrange("a q c -> (a q) c").bitcast(I32))
+        for tile in (tab_rows, w1_rows):
+            nc.vector.memset(tile[scale_rows : P // 2, :].bitcast(I32), 0)
+            nc.vector.memset(tile[P // 2 : P, :].bitcast(I32), 0)
+
         planes = keep.tile([P, K_PASSES, S + H], U8, name="planes", align_bytes=64)
         nc.vector.memset(planes[:].rearrange("p a c -> p (a c)").bitcast(I32), 0)
 
+        for r in range(LIVE_ROWS):
+            nc.sync.dma_start(xs_plane[r:P:QUADRANT, :].bitcast(I32), xs_scales[0, r:BLOCKS:LIVE_ROWS, :].bitcast(I32))
 
         def load_w2(b):
-            raw = stage.tile([P, PACK, K_PASS], F32, name="raw", align_bytes=64)
+            raw = keep.tile([P, PACK, K_PASS], F32, name="w2_raw_%d" % b, tag="raw_%d" % b, align_bytes=64)
             nc.sync.dma_start(raw[:], w2[:, b * K_PASS : (b + 1) * K_PASS].rearrange("(p i) c -> p i c", i=PACK))
             return raw
 
         w2_raw = [load_w2(0)]
-        for quadrant in range(4):
-            nc.sync.dma_start(
-                xs_plane[32 * quadrant : 32 * quadrant + 4, :].bitcast(I32),
-                xs_scales[0, 4 * quadrant : 4 * quadrant + 4, :].bitcast(I32),
-            )
         xs_codes = keep.tile([P, S], I32, name="xs_codes", align_bytes=64)
         nc.sync.dma_start(xs_codes[:], xs_words[0].rearrange("p c i -> p (c i)").bitcast(I32))
         w2_raw.append(load_w2(1))
-        w1_raw = keep.tile([P, K_PASSES, H // 2], I32, name="w1_raw", align_bytes=64)
+        w1_raw = keep.tile([P, K_PASSES, H // 2], I32, name="w1_raw", tag="w1_raw", align_bytes=64)
         nc.sync.dma_start(w1_raw[:], w1_words.rearrange("a p c -> p a c").bitcast(I32))
 
-        gains = keep.tile([P, N_TILES], F32, name="gains")
-        with nc.allow_non_contiguous_dma(reason="one gain a partition"):
-            nc.sync.dma_start(gains[:], gain.rearrange("(i p) -> p i", p=P))
-
-        joined = keep.tile([P, (S + H) // 4], I32, name="joined", align_bytes=64)
-        nc.vector.tensor_copy(
-            joined[0:rows, S // 4 :].rearrange("p (b t g w) -> p b t g w", b=R_PASSES, t=PACK, w=2),
-            w1_rows[0:rows, :].bitcast(I32).rearrange("p (b g t w) -> p b t g w", b=R_PASSES, t=PACK, w=2),
-        )
-        picked_rows = keep.tile([P, S], U8, name="picked_rows", tag="table", align_bytes=64)
+        picked_rows = keep.tile([P, S], U8, name="picked_rows", tag="picked_rows", align_bytes=64)
         nc.vector.tensor_copy(picked_rows[:], tab_rows[:].indirect(offsets[:]))
-        nc.vector.tensor_copy(joined[0:rows, 0 : S // 4], picked_rows[0:rows, :].bitcast(I32))
+        table = [
+            keep.tile([P, T], I32, name="table_0", align_bytes=64),
+            keep.tile([P, T], I32, name="table_1", tag="late_table", align_bytes=64),
+        ]
 
-        table = keep.tile([P, K_PASSES, T], I32, name="table", tag="table", align_bytes=64)
-        for a in range(K_PASSES):
-            for quadrant in range(4):
-                first = 16 * a + 4 * quadrant
-                nc.sync.dma_start(
-                    planes[32 * quadrant : 32 * quadrant + 4, a, :].bitcast(I32), joined[first : first + 4, :]
-                )
-            nc.sync.dma_start(table[:, a, :], tab_words[a].rearrange("p c i -> p (c i)").bitcast(I32))
+        def load_table_and_planes():
+            joined = keep.tile([P, (S + H) // 4], I32, name="joined", tag="raw_0", align_bytes=64)
+            nc.vector.tensor_copy(joined[0:scale_rows, 0 : S // 4], picked_rows[0:scale_rows, :].bitcast(I32))
+            nc.vector.tensor_copy(
+                joined[:, S // 4 :].bitcast(U8).rearrange("p (b t m) -> p b t m", b=R_PASSES, t=PACK),
+                w1_rows[:].rearrange("p (b m t) -> p b t m", b=R_PASSES, t=PACK),
+            )
+            for a in range(K_PASSES):
+                nc.sync.dma_start(table[a][:], tab_words[a].rearrange("p c i -> p (c i)").bitcast(I32))
+                for r in range(LIVE_ROWS):
+                    nc.sync.dma_start(
+                        planes[r:P:QUADRANT, a, :].bitcast(I32),
+                        joined[BLOCKS * a + r : BLOCKS * (a + 1) : LIVE_ROWS, :],
+                    )
 
-        starts = [sum(CHUNKS[:c]) for c in range(len(CHUNKS))]
-        units = [(c, u) for c, width in enumerate(CHUNKS) for u in range(width // UNIT)]
+        def take_bank(number):
+            return psum.tile([P, BANK_COLUMNS], F32, name="bank_%d" % (number % BANKS))
 
-        def abs_out(target, bank):
+        def absolute_values(target, bank):
             nc.scalar.activation(
                 target.rearrange("p (j e t) -> p j t e", t=PACK, e=2),
                 bank[:].rearrange("p (t j e) -> p j t e", t=PACK, e=2),
                 ABS,
             )
 
-        h2 = [keep.tile([P, R_PASSES, PACK * width], BF16, name="h2_%d" % c, align_bytes=64) for c, width in enumerate(CHUNKS)]
+        def chunk_tiles(label):
+            return [
+                keep.tile([P, R_PASSES, PACK * width], BF16, name="%s_%d" % (label, c), align_bytes=64)
+                for c, width in enumerate(CHUNKS)
+            ]
+
+        starts = [sum(CHUNKS[:c]) for c in range(len(CHUNKS))]
+
+        h2 = chunk_tiles("h2")
         for b in range(R_PASSES):
-            w2_bf = stage.tile([P, PACK * K_PASS], BF16, name="w_bf", align_bytes=64)
+            w2_rounded = ring.tile([P, PACK * K_PASS], BF16, name="rounded", align_bytes=64)
             nc.vector.tensor_copy(
-                w2_bf[:].rearrange("p (t g q i) -> p t g i q", t=PACK, q=8, i=PACK),
-                w2_raw[b][:].rearrange("p i (g t q) -> p t g i q", t=PACK, q=8),
+                w2_rounded[:].rearrange("p (t m i) -> p m i t", t=PACK, i=PACK),
+                w2_raw[b][:].rearrange("p i (m t) -> p m i t", t=PACK),
             )
             w2_codes = keep.tile([P, K_PASS], U32, name="w2_codes_%d" % b, align_bytes=64)
             w2_plane = keep.tile([P, K_PASS], U8, name="w2_plane_%d" % b, align_bytes=64)
-            nc.vector.quantize_mx(out=w2_codes[:].bitcast(FP8X4), scales=w2_plane[:], in_=w2_bf[:])
-            for c, u in units:
-                tokens = slice(starts[c] + u * UNIT, starts[c] + (u + 1) * UNIT)
-                bank = psum.tile([P, PACK * UNIT], F32, name="bank")
-                for t in range(PACK):
-                    cols = slice(t * P, (t + 1) * P)
-                    nc.tensor.matmul_mx(
-                        out=bank[:, t * UNIT : (t + 1) * UNIT],
-                        lhsT=w2_codes[:, cols].bitcast(FP8X4),
-                        lhsT_scale=w2_plane[:, cols],
-                        rhs=xs_codes[:, tokens].bitcast(FP8X4),
-                        rhs_scale=xs_plane[:, tokens],
-                        start=True,
-                        stop=True,
-                    )
-                abs_out(h2[c][:, b, u * PACK * UNIT : (u + 1) * PACK * UNIT], bank)
+            nc.vector.quantize_mx(out=w2_codes[:].bitcast(FP8X4), scales=w2_plane[:], in_=w2_rounded[:])
+            if b == 0:
+                load_table_and_planes()
+            for c, width in enumerate(CHUNKS):
+                for u in range(width // UNIT):
+                    token = starts[c] + u * UNIT
+                    bank = take_bank(token // UNIT)
+                    for t in range(PACK):
+                        nc.tensor.matmul_mx(
+                            out=bank[:, t * UNIT : (t + 1) * UNIT],
+                            lhsT=w2_codes[:, t * P : (t + 1) * P].bitcast(FP8X4),
+                            lhsT_scale=w2_plane[:, t * P : (t + 1) * P],
+                            rhs=xs_codes[:, token : token + UNIT].bitcast(FP8X4),
+                            rhs_scale=xs_plane[:, token : token + UNIT],
+                            start=True,
+                            stop=True,
+                        )
+                    absolute_values(h2[c][:, b, u * BANK_COLUMNS : (u + 1) * BANK_COLUMNS], bank)
 
         w1_codes = keep.tile([P, K_PASSES * H // 2], I32, name="w1_codes", align_bytes=64)
         nc.vector.tensor_copy(
-            w1_codes[:].rearrange("p (e t g w) -> p e t g w", t=PACK, g=16, w=4),
-            w1_raw[:].rearrange("p a (b g t w) -> p (a b) t g w", b=R_PASSES, t=PACK, w=4),
+            w1_codes[:].bitcast(U16).rearrange("p (e t m) -> p e t m", t=PACK, m=P),
+            w1_raw[:].rearrange("p a c -> p (a c)").bitcast(U16).rearrange("p (e m t) -> p e t m", t=PACK, m=P),
         )
+
+        gains = keep.tile([P, N_TILES], F32, name="gains", tag="picked_rows", align_bytes=64)
+        with nc.allow_non_contiguous_dma(reason="one gain a partition and tile of output rows"):
+            nc.sync.dma_start(gains[:], gain.rearrange("(i p) -> p i", p=P))
 
         picked = {}
         for a in range(K_PASSES):
-            for half in range(2):
+            for half in range(S // HALF):
                 words = keep.tile([P, HALF], U32, name="picked_%d_%d" % (a, half), align_bytes=64)
-                entries = offsets[:, half * HALF // 16 : (half + 1) * HALF // 16]
-                nc.vector.tensor_copy(words[:], table[:, a, :].bitcast(U32).indirect(entries))
+                entries = offsets[:, half * HALF // LIST_ROWS : (half + 1) * HALF // LIST_ROWS]
+                nc.vector.tensor_copy(words[:], table[a][:].bitcast(U32).indirect(entries))
                 picked[a, half] = words
 
         w3_codes = []
         w3_planes = []
-        for b in range(R_PASSES):
-            raw = stage.tile([P, PACK, N], F32, name="raw", align_bytes=64)
-            by_slot = w3[b * K_PASS : (b + 1) * K_PASS, :].rearrange("(g t q) n -> t g q n", t=PACK, q=8)
-            for t in range(PACK):
-                nc.sync.dma_start(raw[:, t, :], by_slot[t])
-            w3_bf = stage.tile([P, PACK * N], BF16, name="w_bf", align_bytes=64)
+        for b, tag in enumerate(("raw_1", "w1_raw")):
+            raw = keep.tile([P, PACK, N], F32, name="w3_raw_%d" % b, tag=tag, align_bytes=64)
+            nc.sync.dma_start(raw[:], w3[b * K_PASS : (b + 1) * K_PASS, :].rearrange("(p t) n -> p t n", t=PACK))
+            w3_rounded = ring.tile([P, PACK * N], BF16, name="rounded", align_bytes=64)
             nc.vector.tensor_copy(
-                w3_bf[:].rearrange("p (c i t) -> p c t i", i=4, t=PACK),
+                w3_rounded[:].rearrange("p (c i t) -> p c t i", i=4, t=PACK),
                 raw[:].rearrange("p t (c i) -> p c t i", i=4),
             )
             codes = keep.tile([P, N], U32, name="w3_codes_%d" % b, align_bytes=64)
             plane = keep.tile([P, N], U8, name="w3_plane_%d" % b, align_bytes=64)
-            nc.vector.quantize_mx(out=codes[:].bitcast(FP8X4), scales=plane[:], in_=w3_bf[:])
+            nc.vector.quantize_mx(out=codes[:].bitcast(FP8X4), scales=plane[:], in_=w3_rounded[:])
             w3_codes.append(codes)
             w3_planes.append(plane)
 
-        h1 = [keep.tile([P, R_PASSES, PACK * width], BF16, name="h1_%d" % c, align_bytes=64) for c, width in enumerate(CHUNKS)]
+        h1 = chunk_tiles("h1")
         z_codes = []
         z_planes = []
-
-        def overlap(c):
-            width = CHUNKS[c]
+        for c, width in enumerate(CHUNKS):
             for u in range(width // UNIT):
                 token = starts[c] + u * UNIT
                 half, place = divmod(token, HALF)
                 for b in range(R_PASSES):
-                    bank = psum.tile([P, PACK * UNIT], F32, name="bank")
+                    bank = take_bank(R_PASSES * (token // UNIT) + b)
                     for a in range(K_PASSES):
                         for t in range(PACK):
                             column = b * K_PASS + t * P
-                            word = (a * H + column) // 2
+                            first = (a * H + column) // 2
                             nc.tensor.matmul_mx(
                                 out=bank[:, t * UNIT : (t + 1) * UNIT],
-                                lhsT=w1_codes[:, word : word + P // 2].bitcast(FP4X4),
+                                lhsT=w1_codes[:, first : first + P // 2].bitcast(FP4X4),
                                 lhsT_scale=planes[:, a, S + column : S + column + P],
                                 rhs=picked[a, half][:, place : place + UNIT].bitcast(FP8X4),
                                 rhs_scale=planes[:, a, token : token + UNIT],
                                 start=(a == 0 and t == 0),
                                 stop=(a == K_PASSES - 1 and t == PACK - 1),
                             )
-                    abs_out(h1[c][:, b, u * PACK * UNIT : (u + 1) * PACK * UNIT], bank)
-            z = keep.tile([P, R_PASSES, PACK * width], BF16, name="z_%d" % c, align_bytes=64)
+                    absolute_values(h1[c][:, b, u * BANK_COLUMNS : (u + 1) * BANK_COLUMNS], bank)
+            z = ring.tile([P, R_PASSES, PACK * width], BF16, name="rounded", align_bytes=64)
             nc.vector.tensor_tensor(z[:], h1[c][:], h2[c][:], MIN)
             codes = keep.tile([P, R_PASSES * width], U32, name="z_codes_%d" % c, align_bytes=64)
             plane = keep.tile([P, R_PASSES * width], U8, name="z_plane_%d" % c, align_bytes=64)
@@ -198,17 +214,16 @@ def tile_list_cork_taint_overlap_kernel(
             z_planes.append(plane)
 
         out_rows = out.rearrange("(i p) j -> p i j", p=P)
-
-        def scores(c):
-            width = CHUNKS[c]
+        banks_per_chunk = N_TILES // TILES_PER_BANK
+        for c, width in enumerate(CHUNKS):
             result = keep.tile([P, N_TILES, width], F32, name="result_%d" % c, align_bytes=64)
-            per_bank = 2
-            for first in range(0, N_TILES, per_bank):
-                bank = psum.tile([P, PACK * UNIT], F32, name="bank")
-                for i in range(first, first + per_bank):
+            for s in range(banks_per_chunk):
+                bank = take_bank(banks_per_chunk * c + s)
+                tiles = [(TILES_PER_BANK * s + d, bank[:, d * width : (d + 1) * width]) for d in range(TILES_PER_BANK)]
+                for i, sums in tiles:
                     for b in range(R_PASSES):
                         nc.tensor.matmul_mx(
-                            out=bank[:, (i - first) * width : (i - first + 1) * width],
+                            out=sums,
                             lhsT=w3_codes[b][:, i * P : (i + 1) * P].bitcast(FP8X4),
                             lhsT_scale=w3_planes[b][:, i * P : (i + 1) * P],
                             rhs=z_codes[c][:, b * width : (b + 1) * width].bitcast(FP8X4),
@@ -216,16 +231,9 @@ def tile_list_cork_taint_overlap_kernel(
                             start=(b == 0),
                             stop=(b == R_PASSES - 1),
                         )
-                for i in range(first, first + per_bank):
-                    sums = bank[:, (i - first) * width : (i - first + 1) * width]
-                    if c >= len(CHUNKS) - VECTOR_CHUNKS:
+                for i, sums in tiles:
+                    if c >= len(CHUNKS) - SHARED_CHUNKS and s == banks_per_chunk - 1:
                         nc.vector.tensor_scalar(result[:, i, :], sums, gains[:, i : i + 1], None, MULT)
                     else:
                         nc.scalar.activation(result[:, i, :], sums, COPY, scale=gains[:, i : i + 1])
             nc.sync.dma_start(out_rows[:, :, starts[c] : starts[c] + width], result[:])
-
-        for c in range(len(CHUNKS) + LAG):
-            if c < len(CHUNKS):
-                overlap(c)
-            if c >= LAG:
-                scores(c - LAG)

from contextlib import ExitStack

import concourse.mybir as mybir

K, K2, H, N, T, S = 1024, 512, 1024, 512, 4096, 1024
FLOPS = 2 * S * (K * H + K2 * H + H * N)

F32 = mybir.dt.float32
BF16 = mybir.dt.bfloat16
I32 = mybir.dt.int32
U32 = mybir.dt.uint32
U16 = mybir.dt.uint16
U8 = mybir.dt.uint8
FP8X4 = mybir.dt.float8_e4m3fn_x4
FP4X4 = mybir.dt.float4_e2m1fn_x4
ABS = mybir.ActivationFunctionType.Abs
COPY = mybir.ActivationFunctionType.Copy
MIN = mybir.AluOpType.min
MULT = mybir.AluOpType.mult

P = 128
QUADRANT = 32
LIVE_ROWS = 4
PACK = 4
K_PASS = P * PACK
BLOCKS = K_PASS // 32
K_PASSES = K // K_PASS
R_PASSES = H // K_PASS
N_TILES = N // P
LIST_ROWS = 16
BANKS = 8
BANK_COLUMNS = 512
UNIT = BANK_COLUMNS // PACK
HALF = S // 2
CHUNKS = (256, 256, 256, 128, 128)
TILES_PER_BANK = 2
SHARED_CHUNKS = 2


def tile_list_cork_taint_overlap_kernel(
    tc, tab_words, tab_scales, offs, xs_words, xs_scales, w1_words, w1_scales, w2, w3, gain, out
):
    nc = tc.nc
    with ExitStack() as ctx:
        lists = ctx.enter_context(tc.tile_pool(name="lists", bufs=1))
        keep = ctx.enter_context(tc.tile_pool(name="keep", bufs=1))
        ring = ctx.enter_context(tc.tile_pool(name="ring", bufs=2))
        psum = ctx.enter_context(tc.psum_pool(name="psum", bufs=1))

        offsets = lists.tile([P, S // LIST_ROWS], U16, name="offsets")
        nc.sync.dma_start(offsets[:], offs)

        xs_plane = keep.tile([P, S], U8, name="xs_plane", align_bytes=64)
        nc.vector.memset(xs_plane[:].bitcast(I32), 0)

        scale_rows = K_PASSES * BLOCKS
        w1_rows = keep.tile([P, H], U8, name="w1_rows", tag="late_table", align_bytes=64)
        tab_rows = keep.tile([P, T], U8, name="tab_rows", align_bytes=64)
        for tile, scales in ((tab_rows, tab_scales), (w1_rows, w1_scales)):
            nc.sync.dma_start(tile[0:scale_rows, :].bitcast(I32), scales.rearrange("a q c -> (a q) c").bitcast(I32))
        for tile in (tab_rows, w1_rows):
            nc.vector.memset(tile[scale_rows : P // 2, :].bitcast(I32), 0)
            nc.vector.memset(tile[P // 2 : P, :].bitcast(I32), 0)

        planes = keep.tile([P, K_PASSES, S + H], U8, name="planes", align_bytes=64)
        nc.vector.memset(planes[:].rearrange("p a c -> p (a c)").bitcast(I32), 0)

        for r in range(LIVE_ROWS):
            nc.sync.dma_start(xs_plane[r:P:QUADRANT, :].bitcast(I32), xs_scales[0, r:BLOCKS:LIVE_ROWS, :].bitcast(I32))

        def load_w2(b):
            raw = keep.tile([P, PACK, K_PASS], F32, name="w2_raw_%d" % b, tag="raw_%d" % b, align_bytes=64)
            nc.sync.dma_start(raw[:], w2[:, b * K_PASS : (b + 1) * K_PASS].rearrange("(p i) c -> p i c", i=PACK))
            return raw

        w2_raw = [load_w2(0)]
        xs_codes = keep.tile([P, S], I32, name="xs_codes", align_bytes=64)
        nc.sync.dma_start(xs_codes[:], xs_words[0].rearrange("p c i -> p (c i)").bitcast(I32))
        w2_raw.append(load_w2(1))
        w1_raw = keep.tile([P, K_PASSES, H // 2], I32, name="w1_raw", tag="w1_raw", align_bytes=64)
        nc.sync.dma_start(w1_raw[:], w1_words.rearrange("a p c -> p a c").bitcast(I32))

        picked_rows = keep.tile([P, S], U8, name="picked_rows", tag="picked_rows", align_bytes=64)
        nc.vector.tensor_copy(picked_rows[:], tab_rows[:].indirect(offsets[:]))
        table = [
            keep.tile([P, T], I32, name="table_0", align_bytes=64),
            keep.tile([P, T], I32, name="table_1", tag="late_table", align_bytes=64),
        ]

        def load_table_and_planes():
            joined = keep.tile([P, (S + H) // 4], I32, name="joined", tag="raw_0", align_bytes=64)
            nc.vector.tensor_copy(joined[0:scale_rows, 0 : S // 4], picked_rows[0:scale_rows, :].bitcast(I32))
            nc.vector.tensor_copy(
                joined[:, S // 4 :].bitcast(U8).rearrange("p (b t m) -> p b t m", b=R_PASSES, t=PACK),
                w1_rows[:].rearrange("p (b m t) -> p b t m", b=R_PASSES, t=PACK),
            )
            for a in range(K_PASSES):
                nc.sync.dma_start(table[a][:], tab_words[a].rearrange("p c i -> p (c i)").bitcast(I32))
                for r in range(LIVE_ROWS):
                    nc.sync.dma_start(
                        planes[r:P:QUADRANT, a, :].bitcast(I32),
                        joined[BLOCKS * a + r : BLOCKS * (a + 1) : LIVE_ROWS, :],
                    )

        def take_bank(number):
            return psum.tile([P, BANK_COLUMNS], F32, name="bank_%d" % (number % BANKS))

        def absolute_values(target, bank):
            nc.scalar.activation(
                target.rearrange("p (j e t) -> p j t e", t=PACK, e=2),
                bank[:].rearrange("p (t j e) -> p j t e", t=PACK, e=2),
                ABS,
            )

        def chunk_tiles(label):
            return [
                keep.tile([P, R_PASSES, PACK * width], BF16, name="%s_%d" % (label, c), align_bytes=64)
                for c, width in enumerate(CHUNKS)
            ]

        starts = [sum(CHUNKS[:c]) for c in range(len(CHUNKS))]

        h2 = chunk_tiles("h2")
        for b in range(R_PASSES):
            w2_rounded = ring.tile([P, PACK * K_PASS], BF16, name="rounded", align_bytes=64)
            nc.vector.tensor_copy(
                w2_rounded[:].rearrange("p (t m i) -> p m i t", t=PACK, i=PACK),
                w2_raw[b][:].rearrange("p i (m t) -> p m i t", t=PACK),
            )
            w2_codes = keep.tile([P, K_PASS], U32, name="w2_codes_%d" % b, align_bytes=64)
            w2_plane = keep.tile([P, K_PASS], U8, name="w2_plane_%d" % b, align_bytes=64)
            nc.vector.quantize_mx(out=w2_codes[:].bitcast(FP8X4), scales=w2_plane[:], in_=w2_rounded[:])
            if b == 0:
                load_table_and_planes()
            for c, width in enumerate(CHUNKS):
                for u in range(width // UNIT):
                    token = starts[c] + u * UNIT
                    bank = take_bank(token // UNIT)
                    for t in range(PACK):
                        nc.tensor.matmul_mx(
                            out=bank[:, t * UNIT : (t + 1) * UNIT],
                            lhsT=w2_codes[:, t * P : (t + 1) * P].bitcast(FP8X4),
                            lhsT_scale=w2_plane[:, t * P : (t + 1) * P],
                            rhs=xs_codes[:, token : token + UNIT].bitcast(FP8X4),
                            rhs_scale=xs_plane[:, token : token + UNIT],
                            start=True,
                            stop=True,
                        )
                    absolute_values(h2[c][:, b, u * BANK_COLUMNS : (u + 1) * BANK_COLUMNS], bank)

        w1_codes = keep.tile([P, K_PASSES * H // 2], I32, name="w1_codes", align_bytes=64)
        nc.vector.tensor_copy(
            w1_codes[:].bitcast(U16).rearrange("p (e t m) -> p e t m", t=PACK, m=P),
            w1_raw[:].rearrange("p a c -> p (a c)").bitcast(U16).rearrange("p (e m t) -> p e t m", t=PACK, m=P),
        )

        gains = keep.tile([P, N_TILES], F32, name="gains", tag="picked_rows", align_bytes=64)
        with nc.allow_non_contiguous_dma(reason="one gain a partition and tile of output rows"):
            nc.sync.dma_start(gains[:], gain.rearrange("(i p) -> p i", p=P))

        picked = {}
        for a in range(K_PASSES):
            for half in range(S // HALF):
                words = keep.tile([P, HALF], U32, name="picked_%d_%d" % (a, half), align_bytes=64)
                entries = offsets[:, half * HALF // LIST_ROWS : (half + 1) * HALF // LIST_ROWS]
                nc.vector.tensor_copy(words[:], table[a][:].bitcast(U32).indirect(entries))
                picked[a, half] = words

        w3_codes = []
        w3_planes = []
        for b, tag in enumerate(("raw_1", "w1_raw")):
            raw = keep.tile([P, PACK, N], F32, name="w3_raw_%d" % b, tag=tag, align_bytes=64)
            nc.sync.dma_start(raw[:], w3[b * K_PASS : (b + 1) * K_PASS, :].rearrange("(p t) n -> p t n", t=PACK))
            w3_rounded = ring.tile([P, PACK * N], BF16, name="rounded", align_bytes=64)
            nc.vector.tensor_copy(
                w3_rounded[:].rearrange("p (c i t) -> p c t i", i=4, t=PACK),
                raw[:].rearrange("p t (c i) -> p c t i", i=4),
            )
            codes = keep.tile([P, N], U32, name="w3_codes_%d" % b, align_bytes=64)
            plane = keep.tile([P, N], U8, name="w3_plane_%d" % b, align_bytes=64)
            nc.vector.quantize_mx(out=codes[:].bitcast(FP8X4), scales=plane[:], in_=w3_rounded[:])
            w3_codes.append(codes)
            w3_planes.append(plane)

        h1 = chunk_tiles("h1")
        z_codes = []
        z_planes = []
        for c, width in enumerate(CHUNKS):
            for u in range(width // UNIT):
                token = starts[c] + u * UNIT
                half, place = divmod(token, HALF)
                for b in range(R_PASSES):
                    bank = take_bank(R_PASSES * (token // UNIT) + b)
                    for a in range(K_PASSES):
                        for t in range(PACK):
                            column = b * K_PASS + t * P
                            first = (a * H + column) // 2
                            nc.tensor.matmul_mx(
                                out=bank[:, t * UNIT : (t + 1) * UNIT],
                                lhsT=w1_codes[:, first : first + P // 2].bitcast(FP4X4),
                                lhsT_scale=planes[:, a, S + column : S + column + P],
                                rhs=picked[a, half][:, place : place + UNIT].bitcast(FP8X4),
                                rhs_scale=planes[:, a, token : token + UNIT],
                                start=(a == 0 and t == 0),
                                stop=(a == K_PASSES - 1 and t == PACK - 1),
                            )
                    absolute_values(h1[c][:, b, u * BANK_COLUMNS : (u + 1) * BANK_COLUMNS], bank)
            z = ring.tile([P, R_PASSES, PACK * width], BF16, name="rounded", align_bytes=64)
            nc.vector.tensor_tensor(z[:], h1[c][:], h2[c][:], MIN)
            codes = keep.tile([P, R_PASSES * width], U32, name="z_codes_%d" % c, align_bytes=64)
            plane = keep.tile([P, R_PASSES * width], U8, name="z_plane_%d" % c, align_bytes=64)
            nc.vector.quantize_mx(out=codes[:].bitcast(FP8X4), scales=plane[:], in_=z[:].rearrange("p b c -> p (b c)"))
            z_codes.append(codes)
            z_planes.append(plane)

        out_rows = out.rearrange("(i p) j -> p i j", p=P)
        banks_per_chunk = N_TILES // TILES_PER_BANK
        for c, width in enumerate(CHUNKS):
            result = keep.tile([P, N_TILES, width], F32, name="result_%d" % c, align_bytes=64)
            for s in range(banks_per_chunk):
                bank = take_bank(banks_per_chunk * c + s)
                tiles = [(TILES_PER_BANK * s + d, bank[:, d * width : (d + 1) * width]) for d in range(TILES_PER_BANK)]
                for i, sums in tiles:
                    for b in range(R_PASSES):
                        nc.tensor.matmul_mx(
                            out=sums,
                            lhsT=w3_codes[b][:, i * P : (i + 1) * P].bitcast(FP8X4),
                            lhsT_scale=w3_planes[b][:, i * P : (i + 1) * P],
                            rhs=z_codes[c][:, b * width : (b + 1) * width].bitcast(FP8X4),
                            rhs_scale=z_planes[c][:, b * width : (b + 1) * width],
                            start=(b == 0),
                            stop=(b == R_PASSES - 1),
                        )
                for i, sums in tiles:
                    if c >= len(CHUNKS) - SHARED_CHUNKS and s == banks_per_chunk - 1:
                        nc.vector.tensor_scalar(result[:, i, :], sums, gains[:, i : i + 1], None, MULT)
                    else:
                        nc.scalar.activation(result[:, i, :], sums, COPY, scale=gains[:, i : i + 1])
            nc.sync.dma_start(out_rows[:, :, starts[c] : starts[c] + width], result[:])
